import numpy as np
import ml_dtypes


def mxq(x, axis, fmt="e4m3"):
    dtype, down = {"e4m3": (ml_dtypes.float8_e4m3fn, 7), "e5m2": (ml_dtypes.float8_e5m2, 14)}[fmt]
    v = np.moveaxis(np.asarray(x, np.float32).astype(ml_dtypes.bfloat16).astype(np.float64), axis, -1)
    blocks = v.reshape(v.shape[:-1] + (-1, 32))
    amax = np.abs(blocks).max(-1, keepdims=True)
    byte = np.maximum(np.where(amax > 0, np.frexp(amax)[1] - 1 + 127, 0) - down, 1)
    scale = np.exp2(byte - 127.0)
    codes = (blocks / scale).astype(np.float32).astype(dtype).astype(np.float64)
    return np.moveaxis((codes * scale).reshape(v.shape), -1, axis)


WIDE = False


def mx_kscale(k):
    if not WIDE:
        return np.ones(k)
    levels = np.array([30, -30])
    if k % 512:
        return np.exp2(np.random.permutation(np.resize(levels, k // 32))).repeat(32)
    a = np.empty((k // 512, 16))
    for p in range(k // 512):
        a[p, :8] = np.random.permutation(np.resize(levels, 8))
        for g in range(8):
            far = levels[np.abs(levels - a[p, g]) >= 10]
            a[p, g + 8] = far[np.random.randint(len(far))]
    return np.exp2(a.ravel()).repeat(32)


def f64(x):
    return np.asarray(x).astype(np.float64)


def striped(idx):
    return np.tile(np.asarray(idx).reshape(-1, 16).T, (8, 1)).astype(np.uint16)


def unstriped(offs):
    return offs[:16].T.reshape(-1).astype(np.int64)


E2M1 = np.array([0.0, 0.5, 1.0, 1.5, 2.0, 3.0, 4.0, 6.0, -0.0, -0.5, -1.0, -1.5, -2.0, -3.0, -4.0, -6.0])


def pack_weight(w, fmt):
    k, n = w.shape
    w = f64(np.asarray(w, np.float32).astype(ml_dtypes.bfloat16)).reshape(k // 32, 32, n)
    amax = np.abs(w).max(1)
    if fmt == "e4m3":
        byte = np.frexp(amax)[1] - 1 + 127 - 7
    else:
        mant, ex = np.frexp(amax / 6.0)
        byte = np.where(mant > 0.5, ex, ex - 1) + 127
    byte = np.clip(np.where(amax > 0, byte, 1), 1, 254)
    scaled = (w * np.exp2(127.0 - byte)[:, None, :]).reshape(k, n).astype(np.float32)
    by_word = np.ascontiguousarray(scaled.reshape(k // 512, 128, 4, n).transpose(0, 1, 3, 2))
    if fmt == "e4m3":
        words = by_word.astype(ml_dtypes.float8_e4m3fn).view(np.uint8)
    else:
        c = by_word.astype(ml_dtypes.float4_e2m1fn).view(np.uint8) & 0xF
        words = (c[..., 0::2] | (c[..., 1::2] << 4)).reshape(k // 512, 128, 2 * n)
    return np.ascontiguousarray(words), np.ascontiguousarray(byte.astype(np.uint8).reshape(k // 512, 16, n))


def unpack_weight(words, scales, fmt):
    g, _, n = scales.shape
    words = np.ascontiguousarray(words).reshape(g, 128, n, -1)
    if fmt == "e4m3":
        vals = words.view(ml_dtypes.float8_e4m3fn).astype(np.float64)
    else:
        nib = np.empty((g, 128, n, 4), np.uint8)
        nib[..., 0::2] = words & 0xF
        nib[..., 1::2] = words >> 4
        vals = E2M1[nib]
    vals = vals * np.repeat(np.exp2(scales.astype(np.float64) - 127.0), 8, axis=1)[..., None]
    return vals.transpose(0, 1, 3, 2).reshape(g * 512, n)


K, J, N, R, T, V, Q = 512, 512, 256, 256, 1024, 1024, 1024


def setup_inputs():
    n = np.random.standard_normal
    idx = np.random.permutation(T)[:J]
    idx2 = np.random.permutation(V)[:J]
    idx3 = np.random.permutation(Q)[:N]
    fj = mx_kscale(J)
    fk = mx_kscale(K)
    drp = pack_weight(n((K, R)) * 1 / np.sqrt(K) / fk[:, None], "e2m1")
    return {
        "xf": (n((K, T)) * np.random.uniform(0.4, 1.6, (1, T))).astype(np.float32),
        "ca": (np.random.uniform(0.5, 1.5, (J, 1)) * fj[:, None]).astype(np.float32),
        "gt": (n((N, V)) * np.exp(0.5 * n((1, V)))).astype(np.float32),
        "rb": (np.random.uniform(0.5, 1.5, (1, J)) / fj).astype(np.float32),
        "sv": (n((N, V))).astype(np.float32),
        "fkr": (np.random.uniform(0.5, 1.5, (1, K)) * fk).astype(np.float32),
        "dr_words": drp[0],
        "dr_scales": drp[1],
        "old": (0.5 * n((R, Q))).astype(np.float32),
        "offs": striped(idx),
        "offs2": striped(idx2),
        "offs3": striped(idx3),
    }


def reference(xf, ca, gt, rb, sv, fkr, dr_words, dr_scales, old, offs, offs2, offs3):
    idx = unstriped(offs)
    idx2 = unstriped(offs2)
    idx3 = unstriped(offs3)
    dru = unpack_weight(dr_words, dr_scales, "e2m1")
    xj = f64(xf)[:, idx].T
    uj = xj / (np.mean(np.abs(xj), axis=1, keepdims=True) + 0.1) * f64(ca) * f64(fkr)
    gs = f64(gt)[:, idx2] * np.maximum(f64(sv)[:, idx2], 0.0) * f64(rb)
    gj = gs.T
    ujq = mxq(uj, 0, "e5m2")
    gjq = mxq(gj, 0, "e5m2")
    w = ujq.T @ gjq
    wq = mxq(w, 0, "e5m2")
    v2 = dru.T @ wq
    wp = np.zeros((R, Q))
    wp[:, idx3] = v2
    y = 0.05 * wp + f64(old)
    return y

@@ -1,0 +1,229 @@
+from contextlib import ExitStack
+
+import concourse.mybir as mybir
+from concourse.masks import make_identity
+
+K, J, N, R, T, V, Q = 512, 512, 256, 256, 1024, 1024, 1024
+FLOPS = 2 * J * K * N + 2 * K * R * N
+
+F32 = mybir.dt.float32
+BF16 = mybir.dt.bfloat16
+I32 = mybir.dt.int32
+U32 = mybir.dt.uint32
+U16 = mybir.dt.uint16
+U8 = mybir.dt.uint8
+E5M2X4 = mybir.dt.float8_e5m2_x4
+E2M1X4 = mybir.dt.float4_e2m1fn_x4
+ALU = mybir.AluOpType
+ACT = mybir.ActivationFunctionType
+
+P = 128
+PACK = 4
+N_TILES = N // P
+R_TILES = R // P
+STORE_COLS = 512
+X_ON_VECTOR = 352
+
+
+def tile_list_directions_sized_saved_placed_kernel(
+    tc, xf, ca, gt, rb, sv, fkr, dr_words, dr_scales, old, offs, offs2, offs3, out
+):
+    nc = tc.nc
+
+    def gather(engine, dst, window, offsets):
+        if engine == "vector":
+            nc.vector.tensor_copy(dst, window.indirect(offsets))
+        else:
+            nc.scalar.activation(dst, window.indirect(offsets), ACT.Copy)
+
+    def scatter(engine, window, offsets, src):
+        if engine == "vector":
+            nc.vector.tensor_copy(window.indirect(offsets), src)
+        else:
+            nc.scalar.activation(window.indirect(offsets), src, ACT.Copy)
+
+    with ExitStack() as ctx:
+        sb = ctx.enter_context(tc.tile_pool(name="sb", bufs=1))
+        ps = ctx.enter_context(tc.psum_pool(name="ps", bufs=1))
+
+        def quantise(name, src):
+            words = src.shape[1]
+            codes = sb.tile([P, words], U32, name=name + "_codes", align_bytes=64)
+            scales = sb.tile([P, words], U8, name=name + "_scales", align_bytes=64)
+            nc.vector.quantize_mx(
+                out=codes[:].bitcast(E5M2X4), scales=scales[:], in_=src[:].rearrange("p c t -> p (c t)")
+            )
+            return codes, scales
+
+        list_x = sb.tile([P, J // 16], U16, name="list_x")
+        list_g = sb.tile([P, J // 16], U16, name="list_g")
+        list_out = sb.tile([P, N // 16], U16, name="list_out")
+        x_rows = [sb.tile([P, T], F32, name=f"x_rows{i}") for i in range(PACK)]
+        g_rows = [sb.tile([P, V], F32, name=f"g_rows{i}") for i in range(N_TILES)]
+        s_rows = [sb.tile([P, V], F32, name=f"s_rows{i}") for i in range(N_TILES)]
+        old_rows = [sb.tile([P, Q], F32, name=f"old_rows{i}") for i in range(R_TILES)]
+        pages = [sb.tile([P, Q], F32, name=f"page{i}") for i in range(R_TILES)]
+        fkr_col = sb.tile([P, PACK], F32, name="fkr_col")
+        ca_col = sb.tile([P, PACK], F32, name="ca_col")
+        rb_col = sb.tile([P, PACK], F32, name="rb_col")
+        dr_codes = sb.tile([P, 2 * R], U8, name="dr_codes", align_bytes=64)
+        dr_plane = sb.tile([P, R], U8, name="dr_plane", align_bytes=64)
+        ident = sb.tile([P, P], F32, name="ident")
+
+        make_identity(nc, ident[:])
+        nc.vector.memset(dr_plane[:].bitcast(I32), 0)
+        nc.vector.memset(pages[0][:], 0.0)
+        nc.vector.memset(pages[1][:], 0.0)
+        tenth = sb.tile([P, P], F32, name="tenth")
+        nc.scalar.activation(tenth[:], ident[:], ACT.Copy, scale=0.1)
+
+        x_dealt = xf.rearrange("(p i) t -> i p t", i=PACK)
+        nc.sync.dma_start(list_x[:], offs)
+        nc.sync.dma_start(x_rows[0][:], x_dealt[0])
+        nc.sync.dma_start(fkr_col[:], fkr.rearrange("o (p i) -> p (o i)", i=PACK))
+        for i in range(1, PACK):
+            nc.sync.dma_start(x_rows[i][:], x_dealt[i])
+        nc.sync.dma_start(list_g[:], offs2)
+        nc.sync.dma_start(ca_col[:], ca.rearrange("(p t) o -> p (t o)", t=PACK))
+        nc.sync.dma_start(s_rows[0][:], sv[0:P, :])
+        nc.sync.dma_start(g_rows[0][:], gt[0:P, :])
+        nc.sync.dma_start(rb_col[:], rb.rearrange("o (p t) -> p (o t)", t=PACK))
+        nc.sync.dma_start(s_rows[1][:], sv[P : 2 * P, :])
+        nc.sync.dma_start(g_rows[1][:], gt[P : 2 * P, :])
+        nc.sync.dma_start(list_out[:], offs3)
+        nc.sync.dma_start(dr_codes[:].bitcast(I32), dr_words[0].bitcast(I32))
+        for quad in range(4):
+            nc.sync.dma_start(
+                dr_plane[32 * quad : 32 * quad + 4, :].bitcast(I32),
+                dr_scales[0, 4 * quad : 4 * quad + 4, :].bitcast(I32),
+            )
+        for rt in range(R_TILES):
+            nc.sync.dma_start(old_rows[rt][:], old[rt * P : (rt + 1) * P, :])
+
+        abs_sum = ps.tile([P, PACK, P], F32, name="abs_sum", tag="bank_a")
+        for t in range(PACK):
+            nc.tensor.matmul(abs_sum[:, t, :], tenth[:], ident[:], is_transpose=True, start=(t == 0), stop=False)
+        x_banks = []
+        for i in range(PACK):
+            x_picked = sb.tile([P, J], F32, name=f"x_picked{i}")
+            gather("vector", x_picked[:, :X_ON_VECTOR], x_rows[i][:], list_x[:, : X_ON_VECTOR // 16])
+            gather("scalar", x_picked[:, X_ON_VECTOR:], x_rows[i][:], list_x[:, X_ON_VECTOR // 16 :])
+            in_order = x_picked[:].rearrange("k (p t) -> k p t", t=PACK)
+            x_abs = sb.tile([P, PACK, P], F32, name=f"x_abs{i}")
+            nc.scalar.activation(x_abs[:].rearrange("k t p -> k p t"), in_order, ACT.Abs, scale=1.0 / K)
+            for t in range(PACK):
+                nc.tensor.matmul(
+                    abs_sum[:, t, :], x_abs[:, t, :], ident[:], is_transpose=True,
+                    start=False, stop=(i == PACK - 1 and t == PACK - 1),
+                )
+            x_scaled = sb.tile([P, PACK, P], F32, name=f"x_scaled{i}")
+            nc.vector.tensor_scalar(
+                x_scaled[:].rearrange("k t p -> k p t"), in_order, fkr_col[:, i : i + 1], None, ALU.mult
+            )
+            x_bank = ps.tile([P, PACK, P], F32, name=f"x_bank{i}", tag=f"bank_x{i}")
+            for t in range(PACK):
+                nc.tensor.transpose(x_bank[:, t, :], x_scaled[:, t, :], ident[:])
+            x_banks.append(x_bank)
+
+        g_picked, s_picked = [], []
+        for nt in range(N_TILES):
+            s_one = sb.tile([P, J], F32, name=f"s_picked{nt}")
+            gather("vector" if nt == 0 else "scalar", s_one[:], s_rows[nt][:], list_g[:])
+            g_one = sb.tile([P, J], F32, name=f"g_picked{nt}")
+            gather("scalar", g_one[:], g_rows[nt][:], list_g[:])
+            s_picked.append(s_one)
+            g_picked.append(g_one)
+
+        denom = sb.tile([P, PACK], F32, name="denom")
+        nc.vector.tensor_reduce(denom[:], abs_sum[:], mybir.AxisListType.X, ALU.add)
+        inverse = sb.tile([P, PACK], F32, name="inverse")
+        nc.vector.reciprocal(inverse[:], denom[:])
+        slot_factor = sb.tile([P, PACK], F32, name="slot_factor")
+        nc.vector.tensor_tensor(slot_factor[:], inverse[:], ca_col[:], ALU.mult)
+
+        u_bf = sb.tile([P, K, PACK], BF16, name="u_bf", align_bytes=64)
+
+        def round_u(i):
+            nc.vector.tensor_tensor(
+                u_bf[:, i * P : (i + 1) * P, :], x_banks[i][:].rearrange("p t m -> p m t"),
+                slot_factor[:].unsqueeze(1).to_broadcast([P, P, PACK]), ALU.mult,
+            )
+
+        def gate_g(nt):
+            gs = sb.tile([P, PACK, P], F32, name=f"gs{nt}")
+            nc.vector.scalar_tensor_tensor(
+                gs[:].rearrange("n t p -> n p t"),
+                s_picked[nt][:].rearrange("n (p t) -> n p t", t=PACK), 0.0,
+                g_picked[nt][:].rearrange("n (p t) -> n p t", t=PACK), ALU.max, ALU.mult,
+            )
+            g_bank = ps.tile([P, PACK, P], F32, name=f"g_bank{nt}", tag=("bank_g", "bank_a")[nt])
+            for t in range(PACK):
+                nc.tensor.transpose(g_bank[:, t, :], gs[:, t, :], ident[:])
+            return g_bank
+
+        def round_g(nt, g_bank):
+            g_bf = sb.tile([P, P, PACK], BF16, name=f"g_bf{nt}", align_bytes=64)
+            nc.vector.tensor_tensor(
+                g_bf[:], g_bank[:].rearrange("p t n -> p n t"),
+                rb_col[:].unsqueeze(1).to_broadcast([P, P, PACK]), ALU.mult,
+            )
+            return g_bf
+
+        def moment(nt, g_mx):
+            g_codes, g_scales = g_mx
+            w_bank = ps.tile([P, PACK, P], F32, name=f"w_bank{nt}", tag=("bank_w", "bank_x0")[nt])
+            for i in range(PACK):
+                cols = slice(i * P, (i + 1) * P)
+                nc.tensor.matmul_mx(
+                    out=w_bank[:, i, :], lhsT=u_codes[:, cols].bitcast(E5M2X4), lhsT_scale=u_scales[:, cols],
+                    rhs=g_codes[:].bitcast(E5M2X4), rhs_scale=g_scales[:], start=True, stop=True,
+                )
+            w_bf = sb.tile([P, P, PACK], BF16, name=f"w_bf{nt}", align_bytes=64)
+            if nt == 0:
+                nc.scalar.copy(w_bf[:], w_bank[:].rearrange("p i n -> p n i"))
+            else:
+                nc.vector.tensor_copy(w_bf[:], w_bank[:].rearrange("p i n -> p n i"))
+            return w_bf
+
+        def project(nt, w_mx):
+            w_codes, w_scales = w_mx
+            entries = list_out[:, nt * (P // 16) : (nt + 1) * (P // 16)]
+            for rt in range(R_TILES):
+                engine = "vector" if (nt == N_TILES - 1 and rt == 0) else "scalar"
+                v_bank = ps.tile([P, P], F32, name=f"v_bank{nt}{rt}", tag=(("bank_v", "bank_x3"), ("bank_x1", "bank_x2"))[nt][rt])
+                nc.tensor.matmul_mx(
+                    out=v_bank[:],
+                    lhsT=dr_codes[:, 2 * P * rt : 2 * P * (rt + 1)].bitcast(E2M1X4),
+                    lhsT_scale=dr_plane[:, P * rt : P * (rt + 1)],
+                    rhs=w_codes[:].bitcast(E5M2X4), rhs_scale=w_scales[:], start=True, stop=True,
+                )
+                v_sb = sb.tile([P, P], F32, name=f"v_sb{nt}{rt}")
+                if engine == "vector":
+                    nc.vector.tensor_copy(v_sb[:], v_bank[:])
+                else:
+                    nc.scalar.copy(v_sb[:], v_bank[:])
+                scatter(engine, pages[rt][:], entries, v_sb[:])
+
+        round_u(0)
+        round_u(1)
+        g_bank0 = gate_g(0)
+        round_u(2)
+        round_u(3)
+        g_bank1 = gate_g(1)
+        u_codes, u_scales = quantise("u", u_bf)
+        g_bf0 = round_g(0, g_bank0)
+        g_bf1 = round_g(1, g_bank1)
+        w_bf0 = moment(0, quantise("g0", g_bf0))
+        g_mx1 = quantise("g1", g_bf1)
+        project(0, quantise("w0", w_bf0))
+        w_bf1 = moment(1, g_mx1)
+        project(1, quantise("w1", w_bf1))
+
+        for rt in range(R_TILES):
+            for c0 in range(0, Q, STORE_COLS):
+                cols = slice(c0, c0 + STORE_COLS)
+                result = sb.tile([P, STORE_COLS], F32, name=f"result{rt}_{c0}")
+                nc.vector.scalar_tensor_tensor(
+                    result[:], pages[rt][:, cols], 0.05, old_rows[rt][:, cols], ALU.mult, ALU.add
+                )
+                nc.sync.dma_start(out[rt * P : (rt + 1) * P, cols], result[:])

@@ -22,7 +22,7 @@ PACK = 4
 N_TILES = N // P
 R_TILES = R // P
 STORE_COLS = 512
-X_ON_VECTOR = 352
+X_ON_VECTOR = 384
 
 
 def tile_list_directions_sized_saved_placed_kernel(
@@ -64,32 +64,33 @@ def tile_list_directions_sized_saved_placed_kernel(
         old_rows = [sb.tile([P, Q], F32, name=f"old_rows{i}") for i in range(R_TILES)]
         pages = [sb.tile([P, Q], F32, name=f"page{i}") for i in range(R_TILES)]
         fkr_col = sb.tile([P, PACK], F32, name="fkr_col")
-        ca_col = sb.tile([P, PACK], F32, name="ca_col")
+        ca_rows = sb.tile([P, P], F32, name="ca_rows")
         rb_col = sb.tile([P, PACK], F32, name="rb_col")
         dr_codes = sb.tile([P, 2 * R], U8, name="dr_codes", align_bytes=64)
         dr_plane = sb.tile([P, R], U8, name="dr_plane", align_bytes=64)
         ident = sb.tile([P, P], F32, name="ident")
 
-        make_identity(nc, ident[:])
-        nc.vector.memset(dr_plane[:].bitcast(I32), 0)
-        nc.vector.memset(pages[0][:], 0.0)
-        nc.vector.memset(pages[1][:], 0.0)
+        ones = sb.tile([P, P], F32, name="ones")
+        nc.vector.memset(ones[:], 1.0)
         tenth = sb.tile([P, P], F32, name="tenth")
-        nc.scalar.activation(tenth[:], ident[:], ACT.Copy, scale=0.1)
+        nc.scalar.activation(tenth[:], ones[:], ACT.Copy, scale=0.1 / P)
+        make_identity(nc, ident[:])
+        nc.vector.memset(ca_rows[:], 0.0)
+        nc.vector.memset(dr_plane[:].bitcast(I32), 0)
+        nc.gpsimd.memset(pages[0][:], 0.0)
+        nc.gpsimd.memset(pages[1][:], 0.0)
 
         x_dealt = xf.rearrange("(p i) t -> i p t", i=PACK)
         nc.sync.dma_start(list_x[:], offs)
-        nc.sync.dma_start(x_rows[0][:], x_dealt[0])
-        nc.sync.dma_start(fkr_col[:], fkr.rearrange("o (p i) -> p (o i)", i=PACK))
-        for i in range(1, PACK):
+        for i in range(PACK):
             nc.sync.dma_start(x_rows[i][:], x_dealt[i])
+        nc.scalar.dma_start(rb_col[:], rb.rearrange("o (p t) -> p (o t)", t=PACK))
+        nc.scalar.dma_start(fkr_col[:], fkr.rearrange("o (p i) -> p (o i)", i=PACK))
+        nc.scalar.dma_start(ca_rows[0:PACK, :], ca.rearrange("(b p) o -> b (p o)", p=P))
         nc.sync.dma_start(list_g[:], offs2)
-        nc.sync.dma_start(ca_col[:], ca.rearrange("(p t) o -> p (t o)", t=PACK))
-        nc.sync.dma_start(s_rows[0][:], sv[0:P, :])
-        nc.sync.dma_start(g_rows[0][:], gt[0:P, :])
-        nc.sync.dma_start(rb_col[:], rb.rearrange("o (p t) -> p (o t)", t=PACK))
-        nc.sync.dma_start(s_rows[1][:], sv[P : 2 * P, :])
-        nc.sync.dma_start(g_rows[1][:], gt[P : 2 * P, :])
+        for nt in range(N_TILES):
+            nc.sync.dma_start(s_rows[nt][:], sv[nt * P : (nt + 1) * P, :])
+            nc.sync.dma_start(g_rows[nt][:], gt[nt * P : (nt + 1) * P, :])
         nc.sync.dma_start(list_out[:], offs3)
         nc.sync.dma_start(dr_codes[:].bitcast(I32), dr_words[0].bitcast(I32))
         for quad in range(4):
@@ -101,29 +102,27 @@ def tile_list_directions_sized_saved_placed_kernel(
             nc.sync.dma_start(old_rows[rt][:], old[rt * P : (rt + 1) * P, :])
 
         abs_sum = ps.tile([P, PACK, P], F32, name="abs_sum", tag="bank_a")
-        for t in range(PACK):
-            nc.tensor.matmul(abs_sum[:, t, :], tenth[:], ident[:], is_transpose=True, start=(t == 0), stop=False)
-        x_banks = []
+        for b in range(PACK):
+            nc.tensor.matmul(abs_sum[:, b, :], tenth[:], ident[:], is_transpose=True, start=(b == 0), stop=False)
+        x_picked = []
         for i in range(PACK):
-            x_picked = sb.tile([P, J], F32, name=f"x_picked{i}")
-            gather("vector", x_picked[:, :X_ON_VECTOR], x_rows[i][:], list_x[:, : X_ON_VECTOR // 16])
-            gather("scalar", x_picked[:, X_ON_VECTOR:], x_rows[i][:], list_x[:, X_ON_VECTOR // 16 :])
-            in_order = x_picked[:].rearrange("k (p t) -> k p t", t=PACK)
-            x_abs = sb.tile([P, PACK, P], F32, name=f"x_abs{i}")
-            nc.scalar.activation(x_abs[:].rearrange("k t p -> k p t"), in_order, ACT.Abs, scale=1.0 / K)
-            for t in range(PACK):
+            picked = sb.tile([P, J], F32, name=f"x_picked{i}")
+            gather("vector", picked[:, :X_ON_VECTOR], x_rows[i][:], list_x[:, : X_ON_VECTOR // 16])
+            gather("scalar", picked[:, X_ON_VECTOR:], x_rows[i][:], list_x[:, X_ON_VECTOR // 16 :])
+            x_abs = sb.tile([P, J], F32, name=f"x_abs{i}")
+            nc.scalar.activation(x_abs[:], picked[:], ACT.Abs, scale=1.0 / K)
+            for b in range(PACK):
                 nc.tensor.matmul(
-                    abs_sum[:, t, :], x_abs[:, t, :], ident[:], is_transpose=True,
-                    start=False, stop=(i == PACK - 1 and t == PACK - 1),
+                    abs_sum[:, b, :], x_abs[:, b * P : (b + 1) * P], ident[:], is_transpose=True,
+                    start=False, stop=(i == PACK - 1 and b == PACK - 1),
                 )
-            x_scaled = sb.tile([P, PACK, P], F32, name=f"x_scaled{i}")
-            nc.vector.tensor_scalar(
-                x_scaled[:].rearrange("k t p -> k p t"), in_order, fkr_col[:, i : i + 1], None, ALU.mult
-            )
-            x_bank = ps.tile([P, PACK, P], F32, name=f"x_bank{i}", tag=f"bank_x{i}")
-            for t in range(PACK):
-                nc.tensor.transpose(x_bank[:, t, :], x_scaled[:, t, :], ident[:])
-            x_banks.append(x_bank)
+            x_picked.append(picked)
+
+        ca_turned = ps.tile([P, P], F32, name="ca_turned", tag="bank_b")
+        nc.tensor.transpose(ca_turned[:], ca_rows[:], ident[:])
+        rb_spread = ps.tile([P, PACK, P], F32, name="rb_spread", tag="bank_c")
+        for t in range(PACK):
+            nc.tensor.transpose(rb_spread[:, t, :], rb_col[:, t : t + 1].to_broadcast([P, P]), ident[:])
 
         g_picked, s_picked = [], []
         for nt in range(N_TILES):
@@ -136,88 +135,94 @@ def tile_list_directions_sized_saved_placed_kernel(
 
         denom = sb.tile([P, PACK], F32, name="denom")
         nc.vector.tensor_reduce(denom[:], abs_sum[:], mybir.AxisListType.X, ALU.add)
-        inverse = sb.tile([P, PACK], F32, name="inverse")
+        inverse = sb.tile([P, PACK], F32, name="inverse", tag="gate0")
         nc.vector.reciprocal(inverse[:], denom[:])
         slot_factor = sb.tile([P, PACK], F32, name="slot_factor")
-        nc.vector.tensor_tensor(slot_factor[:], inverse[:], ca_col[:], ALU.mult)
+        nc.vector.tensor_tensor(slot_factor[:], inverse[:], ca_turned[:, 0:PACK], ALU.mult)
+        slot_spread = ps.tile([P, PACK, P], F32, name="slot_spread", tag="bank_b")
+        for b in range(PACK):
+            nc.tensor.transpose(slot_spread[:, b, :], slot_factor[:, b : b + 1].to_broadcast([P, P]), ident[:])
 
-        u_bf = sb.tile([P, K, PACK], BF16, name="u_bf", align_bytes=64)
+        def turn_pairs(bank, rounded):
+            words = rounded[:].bitcast(F32)
+            for h in range(2):
+                nc.tensor.transpose(bank[:, h, :], words[:, h::2], ident[:])
 
-        def round_u(i):
-            nc.vector.tensor_tensor(
-                u_bf[:, i * P : (i + 1) * P, :], x_banks[i][:].rearrange("p t m -> p m t"),
-                slot_factor[:].unsqueeze(1).to_broadcast([P, P, PACK]), ALU.mult,
-            )
-
-        def gate_g(nt):
-            gs = sb.tile([P, PACK, P], F32, name=f"gs{nt}")
+        def round_u(i, bank):
+            rounded = sb.tile([P, J], BF16, name=f"u_bf{i}")
             nc.vector.scalar_tensor_tensor(
-                gs[:].rearrange("n t p -> n p t"),
-                s_picked[nt][:].rearrange("n (p t) -> n p t", t=PACK), 0.0,
-                g_picked[nt][:].rearrange("n (p t) -> n p t", t=PACK), ALU.max, ALU.mult,
+                rounded[:], x_picked[i][:], fkr_col[:, i : i + 1],
+                slot_spread[:].rearrange("k b p -> k (b p)"), ALU.mult, ALU.mult,
             )
-            g_bank = ps.tile([P, PACK, P], F32, name=f"g_bank{nt}", tag=("bank_g", "bank_a")[nt])
-            for t in range(PACK):
-                nc.tensor.transpose(g_bank[:, t, :], gs[:, t, :], ident[:])
-            return g_bank
+            turn_pairs(bank, rounded)
 
-        def round_g(nt, g_bank):
-            g_bf = sb.tile([P, P, PACK], BF16, name=f"g_bf{nt}", align_bytes=64)
-            nc.vector.tensor_tensor(
-                g_bf[:], g_bank[:].rearrange("p t n -> p n t"),
-                rb_col[:].unsqueeze(1).to_broadcast([P, P, PACK]), ALU.mult,
+        u_grouped = sb.tile([P, K, PACK], BF16, name="u_grouped", align_bytes=64)
+        g_grouped = sb.tile([P, N, PACK], BF16, name="g_grouped", align_bytes=64)
+
+        def as_words(grouped):
+            return grouped.rearrange("p c t -> p (c t)").bitcast(F32)
+
+        def u_pair(half):
+            bank = ps.tile([P, 2, 2, P], F32, name=f"u_bank{half}", tag=("bank_d", "bank_e")[half])
+            for i in range(2):
+                round_u(2 * half + i, bank[:, i])
+            words = as_words(u_grouped[:, 2 * half * P : 2 * (half + 1) * P, :])
+            nc.scalar.copy(words.rearrange("p (i m h) -> p i m h", i=2, h=2), bank[:].rearrange("p i h m -> p i m h"))
+
+        def gate_s(nt):
+            gate = sb.tile([P, P, PACK], F32, name=f"gate{nt}")
+            nc.vector.scalar_tensor_tensor(
+                gate[:], s_picked[nt][:].rearrange("n (p t) -> n p t", t=PACK), 0.0,
+                rb_spread[:].rearrange("n t p -> n p t"), ALU.max, ALU.mult,
             )
-            return g_bf
+            return gate
 
-        def moment(nt, g_mx):
-            g_codes, g_scales = g_mx
-            w_bank = ps.tile([P, PACK, P], F32, name=f"w_bank{nt}", tag=("bank_w", "bank_x0")[nt])
+        def round_g(nt, gate):
+            rounded = sb.tile([P, J], BF16, name=f"g_bf{nt}")
+            nc.vector.tensor_tensor(rounded[:], g_picked[nt][:], gate[:].rearrange("n p t -> n (p t)"), ALU.mult)
+            bank = ps.tile([P, 2, P], F32, name=f"g_bank{nt}", tag=("bank_f", "bank_g")[nt])
+            turn_pairs(bank, rounded)
+            words = as_words(g_grouped[:, nt * P : (nt + 1) * P, :])
+            nc.scalar.copy(words.rearrange("p (n h) -> p n h", h=2), bank[:].rearrange("p h n -> p n h"))
+
+        round_g(0, gate_s(0))
+        u_pair(0)
+        u_pair(1)
+        round_g(1, gate_s(1))
+        u_codes, u_scales = quantise("u", u_grouped)
+        g_codes, g_scales = quantise("g", g_grouped)
+
+        w_grouped = sb.tile([P, N, PACK], BF16, name="w_grouped", align_bytes=64)
+        for nt in range(N_TILES):
+            n_cols = slice(nt * P, (nt + 1) * P)
+            w_bank = ps.tile([P, PACK, P], F32, name=f"w_bank{nt}", tag=("bank_h", "bank_a")[nt])
             for i in range(PACK):
                 cols = slice(i * P, (i + 1) * P)
                 nc.tensor.matmul_mx(
                     out=w_bank[:, i, :], lhsT=u_codes[:, cols].bitcast(E5M2X4), lhsT_scale=u_scales[:, cols],
-                    rhs=g_codes[:].bitcast(E5M2X4), rhs_scale=g_scales[:], start=True, stop=True,
+                    rhs=g_codes[:, n_cols].bitcast(E5M2X4), rhs_scale=g_scales[:, n_cols], start=True, stop=True,
                 )
-            w_bf = sb.tile([P, P, PACK], BF16, name=f"w_bf{nt}", align_bytes=64)
             if nt == 0:
-                nc.scalar.copy(w_bf[:], w_bank[:].rearrange("p i n -> p n i"))
+                nc.scalar.copy(w_grouped[:, n_cols, :], w_bank[:].rearrange("p i n -> p n i"))
             else:
-                nc.vector.tensor_copy(w_bf[:], w_bank[:].rearrange("p i n -> p n i"))
-            return w_bf
+                nc.vector.tensor_copy(w_grouped[:, n_cols, :], w_bank[:].rearrange("p i n -> p n i"))
+        w_codes, w_scales = quantise("w", w_grouped)
 
-        def project(nt, w_mx):
-            w_codes, w_scales = w_mx
-            entries = list_out[:, nt * (P // 16) : (nt + 1) * (P // 16)]
-            for rt in range(R_TILES):
-                engine = "vector" if (nt == N_TILES - 1 and rt == 0) else "scalar"
-                v_bank = ps.tile([P, P], F32, name=f"v_bank{nt}{rt}", tag=(("bank_v", "bank_x3"), ("bank_x1", "bank_x2"))[nt][rt])
-                nc.tensor.matmul_mx(
-                    out=v_bank[:],
-                    lhsT=dr_codes[:, 2 * P * rt : 2 * P * (rt + 1)].bitcast(E2M1X4),
-                    lhsT_scale=dr_plane[:, P * rt : P * (rt + 1)],
-                    rhs=w_codes[:].bitcast(E5M2X4), rhs_scale=w_scales[:], start=True, stop=True,
-                )
-                v_sb = sb.tile([P, P], F32, name=f"v_sb{nt}{rt}")
-                if engine == "vector":
-                    nc.vector.tensor_copy(v_sb[:], v_bank[:])
-                else:
-                    nc.scalar.copy(v_sb[:], v_bank[:])
-                scatter(engine, pages[rt][:], entries, v_sb[:])
-
-        round_u(0)
-        round_u(1)
-        g_bank0 = gate_g(0)
-        round_u(2)
-        round_u(3)
-        g_bank1 = gate_g(1)
-        u_codes, u_scales = quantise("u", u_bf)
-        g_bf0 = round_g(0, g_bank0)
-        g_bf1 = round_g(1, g_bank1)
-        w_bf0 = moment(0, quantise("g0", g_bf0))
-        g_mx1 = quantise("g1", g_bf1)
-        project(0, quantise("w0", w_bf0))
-        w_bf1 = moment(1, g_mx1)
-        project(1, quantise("w1", w_bf1))
+        for rt in range(R_TILES):
+            engine = ("vector", "scalar")[rt]
+            v_bank = ps.tile([P, N], F32, name=f"v_bank{rt}", tag=("bank_d", "bank_e")[rt])
+            nc.tensor.matmul_mx(
+                out=v_bank[:],
+                lhsT=dr_codes[:, 2 * P * rt : 2 * P * (rt + 1)].bitcast(E2M1X4),
+                lhsT_scale=dr_plane[:, P * rt : P * (rt + 1)],
+                rhs=w_codes[:].bitcast(E5M2X4), rhs_scale=w_scales[:], start=True, stop=True,
+            )
+            v_sb = sb.tile([P, N], F32, name=f"v_sb{rt}")
+            if engine == "vector":
+                nc.vector.tensor_copy(v_sb[:], v_bank[:])
+            else:
+                nc.scalar.copy(v_sb[:], v_bank[:])
+            scatter(engine, pages[rt][:], list_out[:], v_sb[:])
 
         for rt in range(R_TILES):
             for c0 in range(0, Q, STORE_COLS):

@@ -21,8 +21,8 @@ P = 128
 PACK = 4
 N_TILES = N // P
 R_TILES = R // P
-STORE_COLS = 512
-X_ON_VECTOR = 384
+HALF = J // 2
+STORE_PIECES = ((0, 0, 512), (0, 512, 1024), (1, 0, 512), (1, 512, 768), (1, 768, 1024))
 
 
 def tile_list_directions_sized_saved_placed_kernel(
@@ -35,6 +35,10 @@ def tile_list_directions_sized_saved_placed_kernel(
             nc.vector.tensor_copy(dst, window.indirect(offsets))
         else:
             nc.scalar.activation(dst, window.indirect(offsets), ACT.Copy)
+
+    def gather_halves(dst, window, offsets):
+        gather("vector", dst[:, :HALF], window[:], offsets[:, : HALF // 16])
+        gather("scalar", dst[:, HALF:], window[:], offsets[:, HALF // 16 :])
 
     def scatter(engine, window, offsets, src):
         if engine == "vector":
@@ -73,7 +77,7 @@ def tile_list_directions_sized_saved_placed_kernel(
         ones = sb.tile([P, P], F32, name="ones")
         nc.vector.memset(ones[:], 1.0)
         tenth = sb.tile([P, P], F32, name="tenth")
-        nc.scalar.activation(tenth[:], ones[:], ACT.Copy, scale=0.1 / P)
+        nc.scalar.activation(tenth[:], ones[:], ACT.Copy, scale=0.1 * K / P)
         make_identity(nc, ident[:])
         nc.vector.memset(ca_rows[:], 0.0)
         nc.vector.memset(dr_plane[:].bitcast(I32), 0)
@@ -82,15 +86,16 @@ def tile_list_directions_sized_saved_placed_kernel(
 
         x_dealt = xf.rearrange("(p i) t -> i p t", i=PACK)
         nc.sync.dma_start(list_x[:], offs)
+        nc.sync.dma_start(rb_col[:], rb.rearrange("o (p t) -> p (o t)", t=PACK))
         for i in range(PACK):
             nc.sync.dma_start(x_rows[i][:], x_dealt[i])
-        nc.scalar.dma_start(rb_col[:], rb.rearrange("o (p t) -> p (o t)", t=PACK))
-        nc.scalar.dma_start(fkr_col[:], fkr.rearrange("o (p i) -> p (o i)", i=PACK))
-        nc.scalar.dma_start(ca_rows[0:PACK, :], ca.rearrange("(b p) o -> b (p o)", p=P))
+        nc.sync.dma_start(ca_rows[0:PACK, :], ca.rearrange("(b p) o -> b (p o)", p=P))
         nc.sync.dma_start(list_g[:], offs2)
         for nt in range(N_TILES):
-            nc.sync.dma_start(s_rows[nt][:], sv[nt * P : (nt + 1) * P, :])
             nc.sync.dma_start(g_rows[nt][:], gt[nt * P : (nt + 1) * P, :])
+            nc.sync.dma_start(s_rows[nt][:], sv[nt * P : (nt + 1) * P, :])
+            if nt == 0:
+                nc.sync.dma_start(fkr_col[:], fkr.rearrange("o (p i) -> p (o i)", i=PACK))
         nc.sync.dma_start(list_out[:], offs3)
         nc.sync.dma_start(dr_codes[:].bitcast(I32), dr_words[0].bitcast(I32))
         for quad in range(4):
@@ -101,16 +106,25 @@ def tile_list_directions_sized_saved_placed_kernel(
         for rt in range(R_TILES):
             nc.sync.dma_start(old_rows[rt][:], old[rt * P : (rt + 1) * P, :])
 
+        rb_spread = ps.tile([P, PACK, P], F32, name="rb_spread", tag="bank_c")
+        for t in range(PACK):
+            nc.tensor.transpose(rb_spread[:, t, :], rb_col[:, t : t + 1].to_broadcast([P, P]), ident[:])
+
+        rb_row = sb.tile([P, P, PACK], F32, name="rb_row")
+        nc.scalar.copy(rb_row[:], rb_spread[:].rearrange("n t p -> n p t"))
+
         abs_sum = ps.tile([P, PACK, P], F32, name="abs_sum", tag="bank_a")
         for b in range(PACK):
             nc.tensor.matmul(abs_sum[:, b, :], tenth[:], ident[:], is_transpose=True, start=(b == 0), stop=False)
         x_picked = []
         for i in range(PACK):
             picked = sb.tile([P, J], F32, name=f"x_picked{i}")
-            gather("vector", picked[:, :X_ON_VECTOR], x_rows[i][:], list_x[:, : X_ON_VECTOR // 16])
-            gather("scalar", picked[:, X_ON_VECTOR:], x_rows[i][:], list_x[:, X_ON_VECTOR // 16 :])
+            gather_halves(picked, x_rows[i], list_x)
             x_abs = sb.tile([P, J], F32, name=f"x_abs{i}")
-            nc.scalar.activation(x_abs[:], picked[:], ACT.Abs, scale=1.0 / K)
+            nc.vector.scalar_tensor_tensor(
+                x_abs[:, :HALF], picked[:, :HALF], -1.0, picked[:, :HALF], ALU.mult, ALU.max
+            )
+            nc.scalar.activation(x_abs[:, HALF:], picked[:, HALF:], ACT.Abs)
             for b in range(PACK):
                 nc.tensor.matmul(
                     abs_sum[:, b, :], x_abs[:, b * P : (b + 1) * P], ident[:], is_transpose=True,
@@ -120,25 +134,31 @@ def tile_list_directions_sized_saved_placed_kernel(
 
         ca_turned = ps.tile([P, P], F32, name="ca_turned", tag="bank_b")
         nc.tensor.transpose(ca_turned[:], ca_rows[:], ident[:])
-        rb_spread = ps.tile([P, PACK, P], F32, name="rb_spread", tag="bank_c")
-        for t in range(PACK):
-            nc.tensor.transpose(rb_spread[:, t, :], rb_col[:, t : t + 1].to_broadcast([P, P]), ident[:])
 
-        g_picked, s_picked = [], []
-        for nt in range(N_TILES):
-            s_one = sb.tile([P, J], F32, name=f"s_picked{nt}")
-            gather("vector" if nt == 0 else "scalar", s_one[:], s_rows[nt][:], list_g[:])
-            g_one = sb.tile([P, J], F32, name=f"g_picked{nt}")
-            gather("scalar", g_one[:], g_rows[nt][:], list_g[:])
-            s_picked.append(s_one)
-            g_picked.append(g_one)
+        g_picked = [sb.tile([P, J], F32, name=f"g_picked{nt}") for nt in range(N_TILES)]
+        s_picked = [sb.tile([P, J], F32, name=f"s_picked{nt}") for nt in range(N_TILES)]
+        g_weighted = [sb.tile([P, J], F32, name=f"g_weighted{nt}") for nt in range(N_TILES)]
+
+        def weigh_g(nt):
+            nc.gpsimd.tensor_tensor(
+                g_weighted[nt][:], g_picked[nt][:], rb_row[:].rearrange("n p t -> n (p t)"), ALU.mult
+            )
+
+        gather_halves(g_picked[0], g_rows[0], list_g)
+        weigh_g(0)
 
         denom = sb.tile([P, PACK], F32, name="denom")
         nc.vector.tensor_reduce(denom[:], abs_sum[:], mybir.AxisListType.X, ALU.add)
-        inverse = sb.tile([P, PACK], F32, name="inverse", tag="gate0")
-        nc.vector.reciprocal(inverse[:], denom[:])
+        inverse = s_picked[0][:, 0:PACK]
+        nc.vector.reciprocal(inverse, denom[:])
         slot_factor = sb.tile([P, PACK], F32, name="slot_factor")
-        nc.vector.tensor_tensor(slot_factor[:], inverse[:], ca_turned[:, 0:PACK], ALU.mult)
+        nc.vector.scalar_tensor_tensor(slot_factor[:], inverse, float(K), ca_turned[:, 0:PACK], ALU.mult, ALU.mult)
+
+        gather_halves(s_picked[0], s_rows[0], list_g)
+        gather("scalar", g_picked[1][:], g_rows[1][:], list_g[:])
+        weigh_g(1)
+        gather("scalar", s_picked[1][:], s_rows[1][:], list_g[:])
+
         slot_spread = ps.tile([P, PACK, P], F32, name="slot_spread", tag="bank_b")
         for b in range(PACK):
             nc.tensor.transpose(slot_spread[:, b, :], slot_factor[:, b : b + 1].to_broadcast([P, P]), ident[:])
@@ -156,79 +176,76 @@ def tile_list_directions_sized_saved_placed_kernel(
             )
             turn_pairs(bank, rounded)
 
-        u_grouped = sb.tile([P, K, PACK], BF16, name="u_grouped", align_bytes=64)
-        g_grouped = sb.tile([P, N, PACK], BF16, name="g_grouped", align_bytes=64)
-
         def as_words(grouped):
-            return grouped.rearrange("p c t -> p (c t)").bitcast(F32)
+            return grouped[:].rearrange("p c t -> p (c t)").bitcast(F32)
 
         def u_pair(half):
             bank = ps.tile([P, 2, 2, P], F32, name=f"u_bank{half}", tag=("bank_d", "bank_e")[half])
             for i in range(2):
                 round_u(2 * half + i, bank[:, i])
-            words = as_words(u_grouped[:, 2 * half * P : 2 * (half + 1) * P, :])
-            nc.scalar.copy(words.rearrange("p (i m h) -> p i m h", i=2, h=2), bank[:].rearrange("p i h m -> p i m h"))
-
-        def gate_s(nt):
-            gate = sb.tile([P, P, PACK], F32, name=f"gate{nt}")
-            nc.vector.scalar_tensor_tensor(
-                gate[:], s_picked[nt][:].rearrange("n (p t) -> n p t", t=PACK), 0.0,
-                rb_spread[:].rearrange("n t p -> n p t"), ALU.max, ALU.mult,
+            grouped = sb.tile([P, 2 * P, PACK], BF16, name=f"u_grouped{half}", align_bytes=64)
+            nc.scalar.copy(
+                as_words(grouped).rearrange("p (i m h) -> p i m h", i=2, h=2), bank[:].rearrange("p i h m -> p i m h")
             )
-            return gate
+            return grouped
 
-        def round_g(nt, gate):
+        def round_g(nt):
             rounded = sb.tile([P, J], BF16, name=f"g_bf{nt}")
-            nc.vector.tensor_tensor(rounded[:], g_picked[nt][:], gate[:].rearrange("n p t -> n (p t)"), ALU.mult)
+            nc.vector.scalar_tensor_tensor(
+                rounded[:], s_picked[nt][:], 0.0, g_weighted[nt][:], ALU.max, ALU.mult
+            )
             bank = ps.tile([P, 2, P], F32, name=f"g_bank{nt}", tag=("bank_f", "bank_g")[nt])
             turn_pairs(bank, rounded)
-            words = as_words(g_grouped[:, nt * P : (nt + 1) * P, :])
-            nc.scalar.copy(words.rearrange("p (n h) -> p n h", h=2), bank[:].rearrange("p h n -> p n h"))
+            grouped = sb.tile([P, P, PACK], BF16, name=f"g_grouped{nt}", align_bytes=64)
+            nc.scalar.copy(as_words(grouped).rearrange("p (n h) -> p n h", h=2), bank[:].rearrange("p h n -> p n h"))
+            return grouped
 
-        round_g(0, gate_s(0))
-        u_pair(0)
-        u_pair(1)
-        round_g(1, gate_s(1))
-        u_codes, u_scales = quantise("u", u_grouped)
-        g_codes, g_scales = quantise("g", g_grouped)
+        g_grouped0 = round_g(0)
+        u_grouped = [u_pair(half) for half in range(2)]
+        g_grouped1 = round_g(1)
+        g_mx0 = quantise("g0", g_grouped0)
+        u_mx = [quantise(f"u{half}", u_grouped[half]) for half in range(2)]
+        g_mx = [g_mx0, quantise("g1", g_grouped1)]
 
-        w_grouped = sb.tile([P, N, PACK], BF16, name="w_grouped", align_bytes=64)
+        w_grouped = []
         for nt in range(N_TILES):
-            n_cols = slice(nt * P, (nt + 1) * P)
+            g_codes, g_scales = g_mx[nt]
             w_bank = ps.tile([P, PACK, P], F32, name=f"w_bank{nt}", tag=("bank_h", "bank_a")[nt])
             for i in range(PACK):
-                cols = slice(i * P, (i + 1) * P)
+                u_codes, u_scales = u_mx[i // 2]
+                cols = slice((i % 2) * P, (i % 2 + 1) * P)
                 nc.tensor.matmul_mx(
                     out=w_bank[:, i, :], lhsT=u_codes[:, cols].bitcast(E5M2X4), lhsT_scale=u_scales[:, cols],
-                    rhs=g_codes[:, n_cols].bitcast(E5M2X4), rhs_scale=g_scales[:, n_cols], start=True, stop=True,
+                    rhs=g_codes[:].bitcast(E5M2X4), rhs_scale=g_scales[:], start=True, stop=True,
                 )
+            grouped = sb.tile([P, P, PACK], BF16, name=f"w_grouped{nt}", align_bytes=64)
             if nt == 0:
-                nc.scalar.copy(w_grouped[:, n_cols, :], w_bank[:].rearrange("p i n -> p n i"))
+                nc.scalar.copy(grouped[:], w_bank[:].rearrange("p i n -> p n i"))
             else:
-                nc.vector.tensor_copy(w_grouped[:, n_cols, :], w_bank[:].rearrange("p i n -> p n i"))
-        w_codes, w_scales = quantise("w", w_grouped)
+                nc.vector.tensor_copy(grouped[:], w_bank[:].rearrange("p i n -> p n i"))
+            w_grouped.append(grouped)
 
-        for rt in range(R_TILES):
-            engine = ("vector", "scalar")[rt]
-            v_bank = ps.tile([P, N], F32, name=f"v_bank{rt}", tag=("bank_d", "bank_e")[rt])
-            nc.tensor.matmul_mx(
-                out=v_bank[:],
-                lhsT=dr_codes[:, 2 * P * rt : 2 * P * (rt + 1)].bitcast(E2M1X4),
-                lhsT_scale=dr_plane[:, P * rt : P * (rt + 1)],
-                rhs=w_codes[:].bitcast(E5M2X4), rhs_scale=w_scales[:], start=True, stop=True,
-            )
-            v_sb = sb.tile([P, N], F32, name=f"v_sb{rt}")
-            if engine == "vector":
-                nc.vector.tensor_copy(v_sb[:], v_bank[:])
-            else:
-                nc.scalar.copy(v_sb[:], v_bank[:])
-            scatter(engine, pages[rt][:], list_out[:], v_sb[:])
-
-        for rt in range(R_TILES):
-            for c0 in range(0, Q, STORE_COLS):
-                cols = slice(c0, c0 + STORE_COLS)
-                result = sb.tile([P, STORE_COLS], F32, name=f"result{rt}_{c0}")
-                nc.vector.scalar_tensor_tensor(
-                    result[:], pages[rt][:, cols], 0.05, old_rows[rt][:, cols], ALU.mult, ALU.add
+        v_sb = [sb.tile([P, N], F32, name=f"v_sb{rt}") for rt in range(R_TILES)]
+        for nt in range(N_TILES):
+            w_codes, w_scales = quantise(f"w{nt}", w_grouped[nt])
+            for rt in range(R_TILES):
+                v_bank = ps.tile([P, P], F32, name=f"v_bank{nt}{rt}", tag=(("bank_d", "bank_e"), ("bank_f", "bank_g"))[nt][rt])
+                nc.tensor.matmul_mx(
+                    out=v_bank[:],
+                    lhsT=dr_codes[:, 2 * P * rt : 2 * P * (rt + 1)].bitcast(E2M1X4),
+                    lhsT_scale=dr_plane[:, P * rt : P * (rt + 1)],
+                    rhs=w_codes[:].bitcast(E5M2X4), rhs_scale=w_scales[:], start=True, stop=True,
                 )
-                nc.sync.dma_start(out[rt * P : (rt + 1) * P, cols], result[:])
+                if rt == 0:
+                    nc.vector.tensor_copy(v_sb[rt][:, nt * P : (nt + 1) * P], v_bank[:])
+                else:
+                    nc.scalar.copy(v_sb[rt][:, nt * P : (nt + 1) * P], v_bank[:])
+        for rt in range(R_TILES):
+            scatter(("vector", "scalar")[rt], pages[rt][:], list_out[:], v_sb[rt][:])
+
+        for rt, c0, c1 in STORE_PIECES:
+            result = sb.tile([P, c1 - c0], F32, name=f"result{rt}_{c0}")
+            nc.vector.scalar_tensor_tensor(
+                result[:], pages[rt][:, c0:c1], 0.05, old_rows[rt][:, c0:c1], ALU.mult, ALU.add
+            )
+            nc.sync.dma_start(out[rt * P : (rt + 1) * P, c0:c1], result[:])

from contextlib import ExitStack

import concourse.mybir as mybir
from concourse.masks import make_identity

K, J, N, R, T, V, Q = 512, 512, 256, 256, 1024, 1024, 1024
FLOPS = 2 * J * K * N + 2 * K * R * N

F32 = mybir.dt.float32
BF16 = mybir.dt.bfloat16
I32 = mybir.dt.int32
U32 = mybir.dt.uint32
U16 = mybir.dt.uint16
U8 = mybir.dt.uint8
E5M2X4 = mybir.dt.float8_e5m2_x4
E2M1X4 = mybir.dt.float4_e2m1fn_x4
ALU = mybir.AluOpType
ACT = mybir.ActivationFunctionType

P = 128
PACK = 4
N_TILES = N // P
R_TILES = R // P
HALF = J // 2
STORE_PIECES = ((0, 0, 512), (0, 512, 1024), (1, 0, 512), (1, 512, 768), (1, 768, 1024))


def tile_list_directions_sized_saved_placed_kernel(
    tc, xf, ca, gt, rb, sv, fkr, dr_words, dr_scales, old, offs, offs2, offs3, out
):
    nc = tc.nc

    def gather(engine, dst, window, offsets):
        if engine == "vector":
            nc.vector.tensor_copy(dst, window.indirect(offsets))
        else:
            nc.scalar.activation(dst, window.indirect(offsets), ACT.Copy)

    def gather_halves(dst, window, offsets):
        gather("vector", dst[:, :HALF], window[:], offsets[:, : HALF // 16])
        gather("scalar", dst[:, HALF:], window[:], offsets[:, HALF // 16 :])

    def scatter(engine, window, offsets, src):
        if engine == "vector":
            nc.vector.tensor_copy(window.indirect(offsets), src)
        else:
            nc.scalar.activation(window.indirect(offsets), src, ACT.Copy)

    with ExitStack() as ctx:
        sb = ctx.enter_context(tc.tile_pool(name="sb", bufs=1))
        ps = ctx.enter_context(tc.psum_pool(name="ps", bufs=1))

        def quantise(name, src):
            words = src.shape[1]
            codes = sb.tile([P, words], U32, name=name + "_codes", align_bytes=64)
            scales = sb.tile([P, words], U8, name=name + "_scales", align_bytes=64)
            nc.vector.quantize_mx(
                out=codes[:].bitcast(E5M2X4), scales=scales[:], in_=src[:].rearrange("p c t -> p (c t)")
            )
            return codes, scales

        list_x = sb.tile([P, J // 16], U16, name="list_x")
        list_g = sb.tile([P, J // 16], U16, name="list_g")
        list_out = sb.tile([P, N // 16], U16, name="list_out")
        x_rows = [sb.tile([P, T], F32, name=f"x_rows{i}") for i in range(PACK)]
        g_rows = [sb.tile([P, V], F32, name=f"g_rows{i}") for i in range(N_TILES)]
        s_rows = [sb.tile([P, V], F32, name=f"s_rows{i}") for i in range(N_TILES)]
        old_rows = [sb.tile([P, Q], F32, name=f"old_rows{i}") for i in range(R_TILES)]
        pages = [sb.tile([P, Q], F32, name=f"page{i}") for i in range(R_TILES)]
        fkr_col = sb.tile([P, PACK], F32, name="fkr_col")
        ca_rows = sb.tile([P, P], F32, name="ca_rows")
        rb_col = sb.tile([P, PACK], F32, name="rb_col")
        dr_codes = sb.tile([P, 2 * R], U8, name="dr_codes", align_bytes=64)
        dr_plane = sb.tile([P, R], U8, name="dr_plane", align_bytes=64)
        ident = sb.tile([P, P], F32, name="ident")

        ones = sb.tile([P, P], F32, name="ones")
        nc.vector.memset(ones[:], 1.0)
        tenth = sb.tile([P, P], F32, name="tenth")
        nc.scalar.activation(tenth[:], ones[:], ACT.Copy, scale=0.1 * K / P)
        make_identity(nc, ident[:])
        nc.vector.memset(ca_rows[:], 0.0)
        nc.vector.memset(dr_plane[:].bitcast(I32), 0)
        nc.gpsimd.memset(pages[0][:], 0.0)
        nc.gpsimd.memset(pages[1][:], 0.0)

        x_dealt = xf.rearrange("(p i) t -> i p t", i=PACK)
        nc.sync.dma_start(list_x[:], offs)
        nc.sync.dma_start(rb_col[:], rb.rearrange("o (p t) -> p (o t)", t=PACK))
        for i in range(PACK):
            nc.sync.dma_start(x_rows[i][:], x_dealt[i])
        nc.sync.dma_start(ca_rows[0:PACK, :], ca.rearrange("(b p) o -> b (p o)", p=P))
        nc.sync.dma_start(list_g[:], offs2)
        for nt in range(N_TILES):
            nc.sync.dma_start(g_rows[nt][:], gt[nt * P : (nt + 1) * P, :])
            nc.sync.dma_start(s_rows[nt][:], sv[nt * P : (nt + 1) * P, :])
            if nt == 0:
                nc.sync.dma_start(fkr_col[:], fkr.rearrange("o (p i) -> p (o i)", i=PACK))
        nc.sync.dma_start(list_out[:], offs3)
        nc.sync.dma_start(dr_codes[:].bitcast(I32), dr_words[0].bitcast(I32))
        for quad in range(4):
            nc.sync.dma_start(
                dr_plane[32 * quad : 32 * quad + 4, :].bitcast(I32),
                dr_scales[0, 4 * quad : 4 * quad + 4, :].bitcast(I32),
            )
        for rt in range(R_TILES):
            nc.sync.dma_start(old_rows[rt][:], old[rt * P : (rt + 1) * P, :])

        rb_spread = ps.tile([P, PACK, P], F32, name="rb_spread", tag="bank_c")
        for t in range(PACK):
            nc.tensor.transpose(rb_spread[:, t, :], rb_col[:, t : t + 1].to_broadcast([P, P]), ident[:])

        rb_row = sb.tile([P, P, PACK], F32, name="rb_row")
        nc.scalar.copy(rb_row[:], rb_spread[:].rearrange("n t p -> n p t"))

        abs_sum = ps.tile([P, PACK, P], F32, name="abs_sum", tag="bank_a")
        for b in range(PACK):
            nc.tensor.matmul(abs_sum[:, b, :], tenth[:], ident[:], is_transpose=True, start=(b == 0), stop=False)
        x_picked = []
        for i in range(PACK):
            picked = sb.tile([P, J], F32, name=f"x_picked{i}")
            gather_halves(picked, x_rows[i], list_x)
            x_abs = sb.tile([P, J], F32, name=f"x_abs{i}")
            nc.vector.scalar_tensor_tensor(
                x_abs[:, :HALF], picked[:, :HALF], -1.0, picked[:, :HALF], ALU.mult, ALU.max
            )
            nc.scalar.activation(x_abs[:, HALF:], picked[:, HALF:], ACT.Abs)
            for b in range(PACK):
                nc.tensor.matmul(
                    abs_sum[:, b, :], x_abs[:, b * P : (b + 1) * P], ident[:], is_transpose=True,
                    start=False, stop=(i == PACK - 1 and b == PACK - 1),
                )
            x_picked.append(picked)

        ca_turned = ps.tile([P, P], F32, name="ca_turned", tag="bank_b")
        nc.tensor.transpose(ca_turned[:], ca_rows[:], ident[:])

        g_picked = [sb.tile([P, J], F32, name=f"g_picked{nt}") for nt in range(N_TILES)]
        s_picked = [sb.tile([P, J], F32, name=f"s_picked{nt}") for nt in range(N_TILES)]
        g_weighted = [sb.tile([P, J], F32, name=f"g_weighted{nt}") for nt in range(N_TILES)]

        def weigh_g(nt):
            nc.gpsimd.tensor_tensor(
                g_weighted[nt][:], g_picked[nt][:], rb_row[:].rearrange("n p t -> n (p t)"), ALU.mult
            )

        gather_halves(g_picked[0], g_rows[0], list_g)
        weigh_g(0)

        denom = sb.tile([P, PACK], F32, name="denom")
        nc.vector.tensor_reduce(denom[:], abs_sum[:], mybir.AxisListType.X, ALU.add)
        inverse = s_picked[0][:, 0:PACK]
        nc.vector.reciprocal(inverse, denom[:])
        slot_factor = sb.tile([P, PACK], F32, name="slot_factor")
        nc.vector.scalar_tensor_tensor(slot_factor[:], inverse, float(K), ca_turned[:, 0:PACK], ALU.mult, ALU.mult)

        gather_halves(s_picked[0], s_rows[0], list_g)
        gather("scalar", g_picked[1][:], g_rows[1][:], list_g[:])
        weigh_g(1)
        gather("scalar", s_picked[1][:], s_rows[1][:], list_g[:])

        slot_spread = ps.tile([P, PACK, P], F32, name="slot_spread", tag="bank_b")
        for b in range(PACK):
            nc.tensor.transpose(slot_spread[:, b, :], slot_factor[:, b : b + 1].to_broadcast([P, P]), ident[:])

        def turn_pairs(bank, rounded):
            words = rounded[:].bitcast(F32)
            for h in range(2):
                nc.tensor.transpose(bank[:, h, :], words[:, h::2], ident[:])

        def round_u(i, bank):
            rounded = sb.tile([P, J], BF16, name=f"u_bf{i}")
            nc.vector.scalar_tensor_tensor(
                rounded[:], x_picked[i][:], fkr_col[:, i : i + 1],
                slot_spread[:].rearrange("k b p -> k (b p)"), ALU.mult, ALU.mult,
            )
            turn_pairs(bank, rounded)

        def as_words(grouped):
            return grouped[:].rearrange("p c t -> p (c t)").bitcast(F32)

        def u_pair(half):
            bank = ps.tile([P, 2, 2, P], F32, name=f"u_bank{half}", tag=("bank_d", "bank_e")[half])
            for i in range(2):
                round_u(2 * half + i, bank[:, i])
            grouped = sb.tile([P, 2 * P, PACK], BF16, name=f"u_grouped{half}", align_bytes=64)
            nc.scalar.copy(
                as_words(grouped).rearrange("p (i m h) -> p i m h", i=2, h=2), bank[:].rearrange("p i h m -> p i m h")
            )
            return grouped

        def round_g(nt):
            rounded = sb.tile([P, J], BF16, name=f"g_bf{nt}")
            nc.vector.scalar_tensor_tensor(
                rounded[:], s_picked[nt][:], 0.0, g_weighted[nt][:], ALU.max, ALU.mult
            )
            bank = ps.tile([P, 2, P], F32, name=f"g_bank{nt}", tag=("bank_f", "bank_g")[nt])
            turn_pairs(bank, rounded)
            grouped = sb.tile([P, P, PACK], BF16, name=f"g_grouped{nt}", align_bytes=64)
            nc.scalar.copy(as_words(grouped).rearrange("p (n h) -> p n h", h=2), bank[:].rearrange("p h n -> p n h"))
            return grouped

        g_grouped0 = round_g(0)
        u_grouped = [u_pair(half) for half in range(2)]
        g_grouped1 = round_g(1)
        g_mx0 = quantise("g0", g_grouped0)
        u_mx = [quantise(f"u{half}", u_grouped[half]) for half in range(2)]
        g_mx = [g_mx0, quantise("g1", g_grouped1)]

        w_grouped = []
        for nt in range(N_TILES):
            g_codes, g_scales = g_mx[nt]
            w_bank = ps.tile([P, PACK, P], F32, name=f"w_bank{nt}", tag=("bank_h", "bank_a")[nt])
            for i in range(PACK):
                u_codes, u_scales = u_mx[i // 2]
                cols = slice((i % 2) * P, (i % 2 + 1) * P)
                nc.tensor.matmul_mx(
                    out=w_bank[:, i, :], lhsT=u_codes[:, cols].bitcast(E5M2X4), lhsT_scale=u_scales[:, cols],
                    rhs=g_codes[:].bitcast(E5M2X4), rhs_scale=g_scales[:], start=True, stop=True,
                )
            grouped = sb.tile([P, P, PACK], BF16, name=f"w_grouped{nt}", align_bytes=64)
            if nt == 0:
                nc.scalar.copy(grouped[:], w_bank[:].rearrange("p i n -> p n i"))
            else:
                nc.vector.tensor_copy(grouped[:], w_bank[:].rearrange("p i n -> p n i"))
            w_grouped.append(grouped)

        v_sb = [sb.tile([P, N], F32, name=f"v_sb{rt}") for rt in range(R_TILES)]
        for nt in range(N_TILES):
            w_codes, w_scales = quantise(f"w{nt}", w_grouped[nt])
            for rt in range(R_TILES):
                v_bank = ps.tile([P, P], F32, name=f"v_bank{nt}{rt}", tag=(("bank_d", "bank_e"), ("bank_f", "bank_g"))[nt][rt])
                nc.tensor.matmul_mx(
                    out=v_bank[:],
                    lhsT=dr_codes[:, 2 * P * rt : 2 * P * (rt + 1)].bitcast(E2M1X4),
                    lhsT_scale=dr_plane[:, P * rt : P * (rt + 1)],
                    rhs=w_codes[:].bitcast(E5M2X4), rhs_scale=w_scales[:], start=True, stop=True,
                )
                if rt == 0:
                    nc.vector.tensor_copy(v_sb[rt][:, nt * P : (nt + 1) * P], v_bank[:])
                else:
                    nc.scalar.copy(v_sb[rt][:, nt * P : (nt + 1) * P], v_bank[:])
        for rt in range(R_TILES):
            scatter(("vector", "scalar")[rt], pages[rt][:], list_out[:], v_sb[rt][:])

        for rt, c0, c1 in STORE_PIECES:
            result = sb.tile([P, c1 - c0], F32, name=f"result{rt}_{c0}")
            nc.vector.scalar_tensor_tensor(
                result[:], pages[rt][:, c0:c1], 0.05, old_rows[rt][:, c0:c1], ALU.mult, ALU.add
            )
            nc.sync.dma_start(out[rt * P : (rt + 1) * P, c0:c1], result[:])
